import numpy as np
CORES = [50,51,178,179,306,307,434,435]
N = 8
T = 64
ROUTE = [[[5,1,4,7],[6,0,7,3],[4,2,3,1],[2,7,0,5],[1,5,7,6],[4,5,3,6],[6,2,0,5],[0,3,4,5],[7,6,3,4],[0,2,3,4],[7,0,3,4],[0,1,3,4],[2,7,3,4],[3,4,1,6],[4,2,1,3],[0,3,5,1],[3,5,4,6],[7,2,6,1],[6,0,5,4],[6,2,0,4],[7,4,2,3],[6,5,3,1],[1,4,0,2],[7,3,0,5],[7,2,0,5],[6,7,2,1],[0,7,6,4],[2,7,0,4],[4,3,6,5],[1,7,6,3],[2,1,4,3],[2,6,3,5],[2,4,0,6],[1,3,4,2],[0,5,6,1],[4,1,2,7],[4,5,7,2],[0,5,1,2],[5,0,1,3],[4,7,5,0],[4,3,2,5],[3,6,5,2],[6,1,2,3],[3,2,4,7],[7,3,6,2],[4,7,5,0],[1,3,0,4],[4,6,2,3],[5,6,0,3],[2,5,4,3],[5,1,4,3],[5,6,3,2],[6,4,5,3],[6,5,3,2],[0,3,2,6],[3,6,7,5],[1,7,5,0],[2,5,3,0],[5,6,4,7],[7,1,2,4],[0,5,3,1],[7,1,6,3],[0,3,4,7],[2,4,6,7]],[[7,5,2,6],[0,5,4,3],[6,1,0,4],[2,5,4,7],[0,5,7,3],[3,4,1,5],[5,1,6,3],[5,1,6,3],[2,1,0,4],[0,1,6,5],[3,7,4,2],[0,7,3,1],[3,4,0,1],[6,2,7,4],[4,7,5,0],[4,1,6,5],[7,4,5,1],[5,0,3,4],[4,7,0,3],[7,4,2,5],[1,0,5,6],[3,6,0,5],[6,7,3,2],[1,6,7,0],[0,5,1,3],[1,3,4,5],[7,6,4,2],[5,1,3,4],[7,2,5,3],[6,2,3,5],[4,6,0,1],[0,5,4,2],[4,1,5,3],[6,1,4,0],[6,1,5,2],[2,6,4,5],[4,2,5,0],[0,1,4,6],[0,5,2,7],[6,5,0,1],[3,1,7,0],[6,3,7,0],[0,7,5,6],[3,0,2,7],[1,2,5,6],[3,0,4,7],[4,6,5,2],[1,5,4,2],[0,2,6,4],[3,5,6,4],[4,3,0,6],[5,0,7,3],[5,3,4,0],[7,0,3,5],[1,4,7,2],[4,2,3,7],[7,3,6,1],[0,2,3,7],[7,0,6,2],[7,5,0,3],[0,1,7,5],[4,7,1,0],[1,4,3,5],[3,1,2,7]],[[4,6,7,0],[4,1,5,0],[6,1,7,4],[1,7,2,4],[2,4,3,7],[7,6,1,0],[4,5,2,0],[1,2,5,6],[2,6,0,4],[6,3,7,2],[7,1,2,6],[6,0,2,1],[0,4,5,2],[6,4,5,1],[5,3,0,2],[3,6,5,0],[1,5,6,7],[0,2,5,4],[2,5,0,1],[2,1,7,0],[0,5,1,7],[4,0,6,5],[6,2,5,4],[5,0,6,3],[5,7,3,0],[6,1,2,3],[7,1,6,3],[0,7,6,1],[5,0,6,2],[7,6,0,4],[1,4,0,2],[5,6,7,4],[1,0,5,3],[7,0,6,3],[1,4,0,2],[3,7,6,1],[3,1,2,4],[1,2,6,0],[3,6,2,1],[4,5,7,1],[0,5,7,2],[2,0,4,6],[6,5,4,3],[6,0,3,1],[5,3,4,0],[1,0,7,5],[2,1,6,3],[2,6,1,4],[6,0,5,4],[2,4,5,3],[3,0,1,4],[2,7,1,6],[7,2,1,6],[2,0,5,3],[6,1,4,2],[0,3,6,4],[3,7,5,0],[4,3,2,5],[3,0,7,2],[2,0,6,5],[3,7,1,2],[0,4,6,3],[3,2,5,7],[1,6,2,3]],[[5,7,3,2],[5,0,1,2],[0,6,1,4],[1,0,7,5],[6,1,5,0],[1,0,3,7],[7,0,5,4],[6,5,0,3],[2,6,4,0],[3,1,6,0],[2,4,1,0],[4,3,2,1],[4,3,2,6],[7,6,2,5],[7,5,1,0],[6,5,0,7],[1,6,0,3],[7,2,4,0],[2,5,6,4],[6,3,0,7],[0,4,5,1],[5,1,6,3],[6,1,2,0],[3,1,5,6],[3,2,7,1],[5,4,6,1],[2,5,7,4],[5,3,7,1],[1,7,3,6],[5,4,2,6],[1,3,2,4],[1,5,2,6],[0,4,7,2],[5,0,2,6],[6,1,7,2],[2,0,4,1],[5,1,3,7],[2,7,4,5],[3,2,5,0],[6,1,2,4],[4,5,1,2],[6,5,2,0],[7,3,2,5],[5,6,3,4],[5,4,2,0],[1,0,2,7],[7,4,0,5],[2,4,6,5],[7,0,2,1],[0,3,5,4],[4,7,0,2],[1,6,7,5],[5,6,1,2],[5,6,7,1],[5,7,6,1],[4,6,5,2],[6,5,2,1],[0,6,1,7],[0,3,2,1],[2,4,6,3],[2,3,5,1],[2,3,1,0],[0,3,6,1],[2,3,6,5]],[[3,0,1,4],[1,2,3,5],[3,0,1,7],[7,2,0,4],[1,6,2,5],[3,7,6,1],[7,4,6,5],[5,3,0,2],[3,4,6,7],[2,5,3,1],[0,6,1,2],[1,4,5,2],[2,3,5,4],[3,4,1,7],[6,3,0,4],[0,1,5,3],[7,1,2,0],[3,4,1,0],[2,1,7,3],[5,0,1,6],[0,2,3,5],[1,4,2,0],[7,4,1,0],[6,3,4,1],[3,6,0,2],[2,3,7,4],[2,5,6,4],[1,6,3,2],[7,5,4,1],[2,3,4,5],[7,2,4,6],[2,1,7,3],[7,2,5,0],[7,2,6,1],[5,3,4,0],[1,2,6,4],[5,4,3,0],[6,5,0,4],[1,6,2,4],[6,7,0,3],[5,6,7,3],[2,7,1,3],[6,5,4,2],[6,4,2,5],[1,2,7,5],[2,4,7,5],[0,7,1,2],[7,0,6,2],[3,2,7,5],[5,0,2,6],[6,1,0,2],[4,0,3,1],[1,2,0,6],[3,4,2,0],[7,5,3,0],[3,2,6,5],[3,6,0,2],[2,3,1,0],[4,2,3,1],[0,4,3,6],[5,0,7,6],[6,0,4,3],[6,1,5,0],[7,1,6,3]],[[0,7,6,5],[2,7,4,5],[5,7,2,3],[0,2,5,1],[5,0,3,7],[0,7,3,4],[5,3,7,2],[0,5,7,2],[4,6,1,7],[3,6,5,4],[5,4,3,0],[0,7,1,4],[2,3,5,4],[1,5,4,7],[6,3,5,4],[1,7,6,3],[6,0,4,7],[6,2,0,3],[7,3,0,5],[1,7,5,3],[3,4,1,0],[0,5,7,1],[4,2,5,0],[4,2,7,0],[5,2,4,3],[6,1,5,3],[3,6,0,4],[7,3,0,1],[2,6,0,4],[0,3,5,6],[4,6,1,7],[7,4,6,3],[5,7,4,3],[0,1,7,3],[1,7,2,5],[4,6,0,7],[4,0,5,6],[7,4,6,2],[6,3,1,7],[4,2,7,5],[4,6,5,0],[4,6,5,3],[2,7,0,6],[6,1,2,4],[3,6,1,5],[6,7,0,4],[0,3,7,6],[1,4,2,0],[5,0,6,1],[7,6,4,5],[3,2,5,1],[7,2,6,0],[0,6,3,5],[7,5,3,1],[6,0,1,4],[2,4,5,1],[0,3,6,7],[0,2,1,4],[3,4,1,7],[7,4,2,1],[4,2,6,1],[4,7,5,0],[7,2,1,0],[2,0,6,5]],[[6,1,2,4],[3,1,6,5],[1,2,6,0],[2,6,5,1],[2,0,6,4],[3,1,4,2],[3,5,6,4],[2,3,6,4],[6,1,0,4],[3,7,6,1],[1,7,3,5],[5,7,2,0],[0,3,6,4],[3,5,0,7],[3,0,6,1],[2,5,6,1],[3,2,4,1],[7,5,0,2],[7,3,1,6],[2,5,1,4],[4,5,6,1],[0,5,6,4],[2,0,4,3],[3,0,6,4],[4,5,7,0],[1,2,4,0],[5,7,2,0],[0,1,7,6],[0,4,5,2],[1,3,4,0],[7,1,6,0],[5,4,2,7],[5,2,0,7],[3,7,1,6],[6,3,1,4],[7,6,1,0],[6,0,7,4],[7,5,2,4],[1,7,6,2],[1,3,7,6],[6,3,4,2],[0,2,7,5],[1,3,4,2],[3,2,5,6],[6,0,5,7],[6,3,2,1],[1,3,4,7],[5,1,3,6],[2,5,7,3],[3,6,4,0],[7,4,5,1],[5,2,1,4],[5,0,1,2],[5,6,7,2],[3,0,6,4],[4,7,1,5],[2,6,5,4],[4,5,6,1],[0,4,6,1],[7,2,6,3],[1,6,5,3],[1,5,6,7],[0,7,6,4],[3,0,2,4]],[[2,6,4,7],[1,2,5,3],[2,6,4,0],[0,7,2,6],[7,5,2,1],[6,1,7,3],[3,6,2,0],[1,5,3,0],[7,4,3,1],[4,6,3,7],[6,5,2,1],[1,7,5,4],[7,0,3,6],[1,6,0,5],[2,6,0,3],[2,1,0,5],[5,4,3,6],[5,1,0,4],[1,7,3,6],[7,4,6,5],[3,2,4,6],[4,2,1,6],[7,1,3,4],[7,6,1,0],[7,5,4,0],[7,1,6,2],[5,1,4,6],[3,2,5,6],[1,2,7,6],[3,0,7,6],[6,0,7,3],[3,1,5,7],[3,6,0,1],[3,4,1,5],[2,4,7,1],[6,4,3,1],[6,7,4,0],[3,4,1,0],[4,1,6,5],[1,4,0,2],[0,3,4,6],[4,3,6,1],[2,3,7,6],[5,7,3,6],[0,4,7,1],[6,2,7,1],[5,0,6,1],[1,6,2,4],[7,2,3,6],[6,7,1,2],[2,1,4,3],[1,3,6,0],[0,4,6,1],[2,7,6,1],[5,4,7,6],[6,1,3,0],[3,4,1,0],[6,1,7,4],[0,1,6,4],[2,4,3,5],[2,5,1,4],[0,3,1,7],[4,5,0,3],[2,6,7,1]]]
YW = 275
def setup_inputs(rng):
    return {"x": rng.standard_normal((N, 128, T), dtype=np.float32)}
def reference(x):
    y = np.full((N, 128, YW), np.nan, x.dtype)
    fill = [0] * N
    for r in range(N):
        for t in range(T):
            for e in ROUTE[r][t]:
                y[e][:, fill[e]] = x[r][:, t]
                fill[e] += 1
    return {"y": y}

@@ -1,0 +1,185 @@
+from concourse.bass import DstId, RemoteDMATransfer
+
+NT = 64
+MAXW = 4
+SCRATCH = {
+    "xs": ("sbuf", [128, NT], "float32"),
+    "xa": ("sbuf", [128, NT], "float32"),
+    "land": ("sbuf", [128, 275], "float32"),
+}
+SEMAPHORES = ["ld", "xin", "sent", "arr", "st"]
+PLAN = {}
+
+
+def bits(engines):
+    m = 0
+    for e in engines:
+        m |= 1 << e
+    return m
+
+
+def pack(items, load):
+    groups = {}
+    for it in items:
+        groups.setdefault(it[0], []).append(it)
+    chunks = []
+    for w in sorted(groups):
+        off = [it for it in groups[w] if it[5]]
+        on = [it for it in groups[w] if not it[5]]
+        while off or on:
+            a = off[:8]
+            off = off[8:]
+            b = on[:16 - len(a)]
+            on = on[16 - len(a):]
+            chunks.append(a + b)
+    chunks.sort(key=lambda c: -len(c))
+    calls = []
+    for ch in chunks:
+        free = set(range(16))
+        got = []
+        for it in ch:
+            allowed = [e for e in free if (e < 8 or not it[5])]
+            e = min(allowed, key=lambda e: (load[e], -e))
+            free.discard(e)
+            got.append([e])
+        while free:
+            best = None
+            for i, it in enumerate(ch):
+                m = len(got[i])
+                allowed = sorted([e for e in free if (e < 8 or not it[5])], key=lambda e: (load[e], -e))
+                if len(allowed) < m or m >= 16:
+                    continue
+                end = max(load[e] for e in got[i]) + 128 // m
+                new = max(load[e] for e in got[i] + allowed[:m]) + 64 // m
+                if new < end and (best is None or end > best[0]):
+                    best = (end, i, allowed[:m])
+            if best is None:
+                break
+            got[best[1]] += best[2]
+            for e in best[2]:
+                free.discard(e)
+        for i, it in enumerate(ch):
+            for e in got[i]:
+                load[e] += 128 // len(got[i])
+        calls.append([(got[i], ch[i]) for i in range(len(ch))])
+    return calls
+
+
+def build(route, cores, splits):
+    n = len(cores)
+    col = {}
+    cnt = [0] * n
+    for r in range(n):
+        for t in range(NT):
+            for e in route[r][t]:
+                col[(r, t, e)] = None
+    for e in range(n):
+        for r in range(n):
+            for t in range(NT):
+                if (r, t, e) in col:
+                    col[(r, t, e)] = cnt[e]
+                    cnt[e] += 1
+
+    def runs(r, e, lo, hi, buf, off):
+        out = []
+        t = lo
+        while t < hi:
+            if (r, t, e) in col:
+                t0 = t
+                while t < hi and (r, t, e) in col and t - t0 < MAXW:
+                    t += 1
+                out.append((t - t0, buf, t0, cores[e], col[(r, t0, e)], off))
+            else:
+                t += 1
+        return out
+
+    prog = {}
+
+    def core_of(h, k):
+        return cores[2 * h] - cores[2 * h] % 8 + k
+
+    for h in range(4):
+        for k in range(8):
+            prog[core_of(h, k)] = {"items": [], "xin": 0, "sends": [], "load": [0] * 16}
+    HEAD = {(-1, 0): 0, (-1, 1): 4, (1, 0): 1, (1, 1): 6}
+    TAIL = {0: 5, 1: 7}
+    for r in range(n):
+        hr, par = r // 2, r % 2
+        s = splits[r]
+        me = cores[r]
+        partner = cores[r ^ 1]
+        head, tail = [], []
+        for d, eng in ((1, (0, 1, 2, 3)), (-1, (4, 5, 6, 7))):
+            h = (hr + d) % 4
+            hd = (hr + 2) % 4
+            far = 2 * hd + (0 if d == 1 else 1)
+            p = core_of(h, HEAD[(-d, par)])
+            q = core_of(h, TAIL[par])
+            qbuf = "xa" if d == 1 else "xs"
+            head.append((eng, "xa", p))
+            tail.append((eng, qbuf, q))
+            prog[p]["xin"] += 4
+            prog[q]["xin"] += 4
+            for e, off in ((2 * h, False), (2 * h + 1, False), (far, True)):
+                prog[p]["items"] += runs(r, e, 0, s, "xa", off)
+                prog[q]["items"] += runs(r, e, s, NT, qbuf, off)
+        head.append((tuple(range(8, 16)), "xa", partner))
+        tail.append((tuple(range(8, 16)), "xa", partner))
+        prog[partner]["xin"] += 16
+        prog[me]["sends"] = [(0, s, head), (s, NT, tail)]
+        prog[me]["load"] = [64] * 8 + [32] * 8
+        prog[me]["items"] += runs(r, r ^ 1, 0, NT, "xs", False)
+        prog[partner]["items"] += runs(r, r, 0, NT, "xa", False)
+    arr = {c: 0 for c in cores}
+    for c in prog:
+        p = prog[c]
+        p["calls"] = pack(p["items"], p["load"])
+        p["sent"] = sum(len(eng) for call in p["calls"] for eng, it in call)
+        p["sent"] += sum(len(eng) for lo, hi, trs in p["sends"] for eng, b, d in trs)
+        for call in p["calls"]:
+            for eng, it in call:
+                arr[it[3]] += len(eng)
+    for e in range(n):
+        prog[cores[e]]["arr"] = arr[cores[e]]
+        prog[cores[e]]["cnt"] = cnt[e]
+    return prog
+
+
+SPLITS = [43] * 8
+
+
+def rank_program(g, core, T, topo):
+    if "p" not in PLAN:
+        PLAN["p"] = build(T.tables["ROUTE"], list(T.cores), SPLITS)
+    p = PLAN["p"].get(core)
+    if p is None:
+        return
+    sem = T.sem
+
+    def dst(d):
+        rid, pid = topo.addr(d, core)
+        return DstId(rid=rid, pnc=pid)
+
+    rank = T.rank_of(core)
+    if rank is not None:
+        g.sync.dma_start(T.xs[:], T.x[:]).then_inc(sem.ld, 16)
+        g.wait_ge(sem.ld, 16)
+        for lo, hi, trs in p["sends"]:
+            g.remote_dma_fused(
+                [RemoteDMATransfer(dst_ids=[dst(d)], dma_engine_mask=bits(eng), remote_sem=sem.xin,
+                                   src=T.xs[:, lo:hi], dst=T[b][:, lo:hi]) for eng, b, d in trs],
+                local_sem=sem.sent)
+    g.wait_ge(sem.xin, p["xin"])
+    for call in p["calls"]:
+        g.remote_dma_fused(
+            [RemoteDMATransfer(dst_ids=[dst(it[3])], dma_engine_mask=bits(eng), remote_sem=sem.arr,
+                               src=T[it[1]][:, it[2]:it[2] + it[0]], dst=T.land[:, it[4]:it[4] + it[0]])
+             for eng, it in call],
+            local_sem=sem.sent)
+    if rank is not None:
+        n = p["cnt"]
+        g.sync.wait_ge(sem.arr, p["arr"])
+        g.sync.dma_start(T.y[:, 0:n], T.land[:, 0:n]).then_inc(sem.st, 16)
+        g.wait_ge(sem.arr, p["arr"])
+        g.wait_ge(sem.st, 16)
+    g.wait_ge(sem.sent, p["sent"])

@@ -1,14 +1,23 @@
 from concourse.bass import DstId, RemoteDMATransfer
 
 NT = 64
-MAXW = 4
 SCRATCH = {
     "xs": ("sbuf", [128, NT], "float32"),
     "xa": ("sbuf", [128, NT], "float32"),
+    "xb": ("sbuf", [128, NT], "float32"),
     "land": ("sbuf", [128, 275], "float32"),
 }
 SEMAPHORES = ["ld", "xin", "sent", "arr", "st"]
 PLAN = {}
+SPLITS = [[[40, 49, 62], [40, 52, 58], [38, 47, 55], [32, 46, 56], [32, 45, 56], [36, 45, 59], [35, 49, 57], [33, 52, 60]],
+          [[34, 44, 54], [38, 48, 55], [38, 51, 60], [31, 49, 59], [38, 44, 54], [31, 43, 54], [38, 47, 54], [31, 51, 62]],
+          [[37, 47, 60], [41, 50, 55], [42, 49, 57], [41, 54, 55], [40, 47, 61], [42, 53, 54], [37, 54, 60], [35, 55, 61]],
+          [[39, 47, 55], [39, 49, 59], [36, 46, 57], [39, 49, 54], [34, 45, 57], [31, 48, 58], [32, 42, 51], [39, 49, 56]],
+          [[35, 44, 55], [31, 43, 57], [29, 51, 55], [37, 45, 60], [34, 47, 60], [35, 48, 58], [33, 48, 55], [34, 43, 60]],
+          [[43, 45, 56], [43, 51, 62], [36, 52, 59], [38, 51, 56], [44, 51, 54], [37, 48, 56], [39, 53, 61], [36, 50, 57]],
+          [[37, 51, 59], [37, 48, 60], [36, 50, 58], [33, 45, 53], [33, 45, 60], [40, 47, 55], [37, 51, 55], [34, 48, 54]],
+          [[35, 53, 59], [40, 49, 62], [38, 52, 56], [35, 46, 55], [42, 46, 61], [36, 52, 59], [37, 51, 56], [37, 50, 61]]]
+TRIES = 24
 
 
 def bits(engines):
@@ -18,7 +27,7 @@ def bits(engines):
     return m
 
 
-def pack(items, load):
+def pack_once(items, load, rnd):
     groups = {}
     for it in items:
         groups.setdefault(it[0], []).append(it)
@@ -26,13 +35,14 @@ def pack(items, load):
     for w in sorted(groups):
         off = [it for it in groups[w] if it[5]]
         on = [it for it in groups[w] if not it[5]]
+        cap = (16, 16, 12, 8)[rnd(4)]
         while off or on:
-            a = off[:8]
-            off = off[8:]
-            b = on[:16 - len(a)]
-            on = on[16 - len(a):]
+            a = off[:min(8, cap)]
+            off = off[len(a):]
+            b = on[:cap - len(a)]
+            on = on[len(b):]
             chunks.append(a + b)
-    chunks.sort(key=lambda c: -len(c))
+    chunks.sort(key=lambda c: -len(c) + rnd(5))
     calls = []
     for ch in chunks:
         free = set(range(16))
@@ -65,18 +75,31 @@ def pack(items, load):
     return calls
 
 
-def build(route, cores, splits):
+def pack(items, load0, tries):
+    state = [12345]
+
+    def rnd(n):
+        state[0] = (state[0] * 1103515245 + 12345) % 2147483648
+        return (state[0] >> 8) % n
+
+    best = None
+    for k in range(tries):
+        load = list(load0)
+        calls = pack_once(items, load, rnd if k else (lambda n: 0))
+        score = max(load) + 3 * len(calls)
+        if best is None or score < best[0]:
+            best = (score, calls, load)
+    return best[1], best[2]
+
+
+def build(route, cores, splits, tries):
     n = len(cores)
     col = {}
     cnt = [0] * n
-    for r in range(n):
-        for t in range(NT):
-            for e in route[r][t]:
-                col[(r, t, e)] = None
     for e in range(n):
         for r in range(n):
             for t in range(NT):
-                if (r, t, e) in col:
+                if e in route[r][t]:
                     col[(r, t, e)] = cnt[e]
                     cnt[e] += 1
 
@@ -86,7 +109,7 @@ def build(route, cores, splits):
         while t < hi:
             if (r, t, e) in col:
                 t0 = t
-                while t < hi and (r, t, e) in col and t - t0 < MAXW:
+                while t < hi and (r, t, e) in col:
                     t += 1
                 out.append((t - t0, buf, t0, cores[e], col[(r, t0, e)], off))
             else:
@@ -95,45 +118,56 @@ def build(route, cores, splits):
 
     prog = {}
 
-    def core_of(h, k):
-        return cores[2 * h] - cores[2 * h] % 8 + k
+    def core_of(h, k, chip=6):
+        return cores[2 * h] - cores[2 * h] % 8 + (chip - 6) * 8 + k
 
     for h in range(4):
         for k in range(8):
-            prog[core_of(h, k)] = {"items": [], "xin": 0, "sends": [], "load": [0] * 16}
+            prog[core_of(h, k)] = {"items": [], "xin": 0, "sends": [], "load": [0] * 16, "A": 0}
+            prog[core_of(h, k, 4)] = {"items": [], "xin": 0, "sends": [], "load": [0] * 16, "A": 0}
     HEAD = {(-1, 0): 0, (-1, 1): 4, (1, 0): 1, (1, 1): 6}
     TAIL = {0: 5, 1: 7}
+    LO, HI, UP = (0, 1, 2, 3), (4, 5, 6, 7), tuple(range(8, 16))
     for r in range(n):
         hr, par = r // 2, r % 2
-        s = splits[r]
-        me = cores[r]
-        partner = cores[r ^ 1]
-        head, tail = [], []
-        for d, eng in ((1, (0, 1, 2, 3)), (-1, (4, 5, 6, 7))):
-            h = (hr + d) % 4
-            hd = (hr + 2) % 4
-            far = 2 * hd + (0 if d == 1 else 1)
-            p = core_of(h, HEAD[(-d, par)])
-            q = core_of(h, TAIL[par])
-            qbuf = "xa" if d == 1 else "xs"
-            head.append((eng, "xa", p))
-            tail.append((eng, qbuf, q))
-            prog[p]["xin"] += 4
-            prog[q]["xin"] += 4
-            for e, off in ((2 * h, False), (2 * h + 1, False), (far, True)):
-                prog[p]["items"] += runs(r, e, 0, s, "xa", off)
-                prog[q]["items"] += runs(r, e, s, NT, qbuf, off)
-        head.append((tuple(range(8, 16)), "xa", partner))
-        tail.append((tuple(range(8, 16)), "xa", partner))
-        prog[partner]["xin"] += 16
-        prog[me]["sends"] = [(0, s, head), (s, NT, tail)]
-        prog[me]["load"] = [64] * 8 + [32] * 8
-        prog[me]["items"] += runs(r, r ^ 1, 0, NT, "xs", False)
-        prog[partner]["items"] += runs(r, r, 0, NT, "xa", False)
+        me, partner = cores[r], cores[r ^ 1]
+        hd, hc = (hr + 2) % 4, hr ^ 3
+        for e in range(n):
+            he = e // 2
+            s1, s2, s3 = splits[r][e]
+            if he == hr:
+                hold = [(partner, "xa") if e == r else (me, "xs"), (core_of(hr, TAIL[par]), "xb")]
+                off = False
+            else:
+                h = he if he != hd else (hr + (1 if e % 2 == 0 else 3)) % 4
+                d = 1 if h == (hr + 1) % 4 else -1
+                hold = [(core_of(h, HEAD[(-d, par)]), "xa"), (core_of(h, TAIL[par]), "xa" if d == 1 else "xs")]
+                off = he == hd
+            hx, k0 = (hr, 0) if he // 2 == hr // 2 else (hc, 4)
+            prog[hold[0][0]]["items"] += runs(r, e, 0, s1, hold[0][1], off)
+            prog[hold[1][0]]["items"] += runs(r, e, s1, s2, hold[1][1], off)
+            prog[core_of(hx, k0 + 2 * par, 4)]["items"] += runs(r, e, s2, s3, "xa", True)
+            prog[core_of(hx, k0 + 2 * par + 1, 4)]["items"] += runs(r, e, s3, NT, "xa", True)
+        cut = [0] + [min(splits[r][e][i] for e in range(n)) for i in range(3)]
+        end = [max(splits[r][e][i] for e in range(n)) for i in range(3)] + [NT]
+        hp, hm = (hr + 1) % 4, (hr + 3) % 4
+        trs = [[(LO, "xa", core_of(hp, HEAD[(-1, par)])), (HI, "xa", core_of(hm, HEAD[(1, par)])), (UP, "xa", partner)],
+               [(LO, "xa", core_of(hp, TAIL[par])), (HI, "xs", core_of(hm, TAIL[par])), (UP, "xb", core_of(hr, TAIL[par]))],
+               [(LO, "xa", core_of(hr, 2 * par, 4)), (HI, "xa", core_of(hc, 4 + 2 * par, 4))],
+               [(LO, "xa", core_of(hr, 2 * par + 1, 4)), (HI, "xa", core_of(hc, 5 + 2 * par, 4))]]
+        prog[me]["sends"] = [(cut[i], end[i], trs[i]) for i in range(4)]
+        prog[me]["load"] = [128] * 8 + [32] * 8
+        for i in range(4):
+            for eng, b, d in trs[i]:
+                prog[d]["xin"] += len(eng)
+                if d != partner:
+                    prog[d]["A"] = 32 * (i + 1)
+    if not tries:
+        return prog
     arr = {c: 0 for c in cores}
     for c in prog:
         p = prog[c]
-        p["calls"] = pack(p["items"], p["load"])
+        p["calls"], p["load"] = pack(p["items"], p["load"], tries)
         p["sent"] = sum(len(eng) for call in p["calls"] for eng, it in call)
         p["sent"] += sum(len(eng) for lo, hi, trs in p["sends"] for eng, b, d in trs)
         for call in p["calls"]:
@@ -145,12 +179,9 @@ def build(route, cores, splits):
     return prog
 
 
-SPLITS = [43] * 8
-
-
 def rank_program(g, core, T, topo):
     if "p" not in PLAN:
-        PLAN["p"] = build(T.tables["ROUTE"], list(T.cores), SPLITS)
+        PLAN["p"] = build(T.tables["ROUTE"], list(T.cores), SPLITS, TRIES)
     p = PLAN["p"].get(core)
     if p is None:
         return

@@ -9,15 +9,15 @@ SCRATCH = {
 }
 SEMAPHORES = ["ld", "xin", "sent", "arr", "st"]
 PLAN = {}
-SPLITS = [[[40, 49, 62], [40, 52, 58], [38, 47, 55], [32, 46, 56], [32, 45, 56], [36, 45, 59], [35, 49, 57], [33, 52, 60]],
-          [[34, 44, 54], [38, 48, 55], [38, 51, 60], [31, 49, 59], [38, 44, 54], [31, 43, 54], [38, 47, 54], [31, 51, 62]],
-          [[37, 47, 60], [41, 50, 55], [42, 49, 57], [41, 54, 55], [40, 47, 61], [42, 53, 54], [37, 54, 60], [35, 55, 61]],
-          [[39, 47, 55], [39, 49, 59], [36, 46, 57], [39, 49, 54], [34, 45, 57], [31, 48, 58], [32, 42, 51], [39, 49, 56]],
-          [[35, 44, 55], [31, 43, 57], [29, 51, 55], [37, 45, 60], [34, 47, 60], [35, 48, 58], [33, 48, 55], [34, 43, 60]],
-          [[43, 45, 56], [43, 51, 62], [36, 52, 59], [38, 51, 56], [44, 51, 54], [37, 48, 56], [39, 53, 61], [36, 50, 57]],
-          [[37, 51, 59], [37, 48, 60], [36, 50, 58], [33, 45, 53], [33, 45, 60], [40, 47, 55], [37, 51, 55], [34, 48, 54]],
-          [[35, 53, 59], [40, 49, 62], [38, 52, 56], [35, 46, 55], [42, 46, 61], [36, 52, 59], [37, 51, 56], [37, 50, 61]]]
-TRIES = 24
+SPLITS = [[[37, 49, 62], [40, 52, 58], [38, 46, 58], [34, 46, 56], [30, 44, 56], [36, 46, 59], [37, 47, 58], [34, 50, 60]],
+          [[34, 44, 54], [36, 48, 55], [38, 51, 59], [32, 47, 59], [38, 44, 54], [31, 44, 57], [37, 47, 55], [31, 50, 59]],
+          [[36, 48, 58], [41, 50, 56], [42, 50, 61], [41, 54, 59], [40, 47, 61], [42, 53, 56], [37, 51, 58], [33, 53, 61]],
+          [[39, 47, 55], [39, 47, 59], [36, 47, 57], [36, 50, 53], [33, 45, 55], [31, 46, 57], [32, 46, 53], [39, 49, 56]],
+          [[35, 45, 55], [33, 45, 59], [29, 45, 55], [37, 45, 60], [34, 47, 58], [35, 48, 58], [33, 46, 55], [34, 44, 59]],
+          [[41, 45, 55], [39, 51, 61], [38, 52, 56], [38, 47, 56], [47, 51, 54], [37, 48, 56], [40, 53, 58], [40, 50, 60]],
+          [[37, 48, 56], [40, 48, 60], [36, 50, 58], [33, 45, 54], [33, 45, 60], [37, 47, 55], [37, 50, 55], [36, 48, 54]],
+          [[35, 51, 58], [40, 49, 60], [38, 51, 58], [35, 48, 57], [42, 49, 61], [33, 49, 58], [37, 51, 57], [37, 50, 62]]]
+TRIES = 40
 
 
 def bits(engines):
@@ -75,18 +75,22 @@ def pack_once(items, load, rnd):
     return calls
 
 
-def pack(items, load0, tries):
-    state = [12345]
+def dice(seed):
+    state = [seed * 7919 + 1]
 
     def rnd(n):
         state[0] = (state[0] * 1103515245 + 12345) % 2147483648
         return (state[0] >> 8) % n
 
+    return rnd
+
+
+def pack(items, load0, tries):
     best = None
     for k in range(tries):
         load = list(load0)
-        calls = pack_once(items, load, rnd if k else (lambda n: 0))
-        score = max(load) + 3 * len(calls)
+        calls = pack_once(items, load, dice(k) if k else (lambda n: 0))
+        score = max(load) + 4 * len(calls)
         if best is None or score < best[0]:
             best = (score, calls, load)
     return best[1], best[2]
@@ -132,6 +136,13 @@ def build(route, cores, splits, tries):
         hr, par = r // 2, r % 2
         me, partner = cores[r], cores[r ^ 1]
         hd, hc = (hr + 2) % 4, hr ^ 3
+        need = {}
+
+        def give(i, c, buf, e, lo, hi, off):
+            prog[c]["items"] += runs(r, e, lo, hi, buf, off)
+            a, b = need.get((i, c), (NT, 0))
+            need[(i, c)] = (min(a, lo), max(b, hi))
+
         for e in range(n):
             he = e // 2
             s1, s2, s3 = splits[r][e]
@@ -144,18 +155,20 @@ def build(route, cores, splits, tries):
                 hold = [(core_of(h, HEAD[(-d, par)]), "xa"), (core_of(h, TAIL[par]), "xa" if d == 1 else "xs")]
                 off = he == hd
             hx, k0 = (hr, 0) if he // 2 == hr // 2 else (hc, 4)
-            prog[hold[0][0]]["items"] += runs(r, e, 0, s1, hold[0][1], off)
-            prog[hold[1][0]]["items"] += runs(r, e, s1, s2, hold[1][1], off)
-            prog[core_of(hx, k0 + 2 * par, 4)]["items"] += runs(r, e, s2, s3, "xa", True)
-            prog[core_of(hx, k0 + 2 * par + 1, 4)]["items"] += runs(r, e, s3, NT, "xa", True)
-        cut = [0] + [min(splits[r][e][i] for e in range(n)) for i in range(3)]
-        end = [max(splits[r][e][i] for e in range(n)) for i in range(3)] + [NT]
+            give(0, hold[0][0], hold[0][1], e, 0, s1, off)
+            give(1, hold[1][0], hold[1][1], e, s1, s2, off)
+            give(2, core_of(hx, k0 + 2 * par, 4), "xa", e, s2, s3, True)
+            give(3, core_of(hx, k0 + 2 * par + 1, 4), "xa", e, s3, NT, True)
         hp, hm = (hr + 1) % 4, (hr + 3) % 4
         trs = [[(LO, "xa", core_of(hp, HEAD[(-1, par)])), (HI, "xa", core_of(hm, HEAD[(1, par)])), (UP, "xa", partner)],
                [(LO, "xa", core_of(hp, TAIL[par])), (HI, "xs", core_of(hm, TAIL[par])), (UP, "xb", core_of(hr, TAIL[par]))],
                [(LO, "xa", core_of(hr, 2 * par, 4)), (HI, "xa", core_of(hc, 4 + 2 * par, 4))],
                [(LO, "xa", core_of(hr, 2 * par + 1, 4)), (HI, "xa", core_of(hc, 5 + 2 * par, 4))]]
-        prog[me]["sends"] = [(cut[i], end[i], trs[i]) for i in range(4)]
+        sends = []
+        for i in range(4):
+            wid = max(need[(i, d)][1] - need[(i, d)][0] for eng, b, d in trs[i])
+            sends.append([(eng, b, d, min(need[(i, d)][0], NT - wid), wid) for eng, b, d in trs[i]])
+        prog[me]["sends"] = sends
         prog[me]["load"] = [128] * 8 + [32] * 8
         for i in range(4):
             for eng, b, d in trs[i]:
@@ -169,7 +182,7 @@ def build(route, cores, splits, tries):
         p = prog[c]
         p["calls"], p["load"] = pack(p["items"], p["load"], tries)
         p["sent"] = sum(len(eng) for call in p["calls"] for eng, it in call)
-        p["sent"] += sum(len(eng) for lo, hi, trs in p["sends"] for eng, b, d in trs)
+        p["sent"] += sum(len(tr[0]) for trs in p["sends"] for tr in trs)
         for call in p["calls"]:
             for eng, it in call:
                 arr[it[3]] += len(eng)
@@ -195,10 +208,10 @@ def rank_program(g, core, T, topo):
     if rank is not None:
         g.sync.dma_start(T.xs[:], T.x[:]).then_inc(sem.ld, 16)
         g.wait_ge(sem.ld, 16)
-        for lo, hi, trs in p["sends"]:
+        for trs in p["sends"]:
             g.remote_dma_fused(
                 [RemoteDMATransfer(dst_ids=[dst(d)], dma_engine_mask=bits(eng), remote_sem=sem.xin,
-                                   src=T.xs[:, lo:hi], dst=T[b][:, lo:hi]) for eng, b, d in trs],
+                                   src=T.xs[:, lo:lo + w], dst=T[b][:, lo:lo + w]) for eng, b, d, lo, w in trs],
                 local_sem=sem.sent)
     g.wait_ge(sem.xin, p["xin"])
     for call in p["calls"]:

from concourse.bass import DstId, RemoteDMATransfer

NT = 64
SCRATCH = {
    "xs": ("sbuf", [128, NT], "float32"),
    "xa": ("sbuf", [128, NT], "float32"),
    "xb": ("sbuf", [128, NT], "float32"),
    "land": ("sbuf", [128, 275], "float32"),
}
SEMAPHORES = ["ld", "xin", "sent", "arr", "st"]
PLAN = {}
SPLITS = [[[37, 49, 62], [40, 52, 58], [38, 46, 58], [34, 46, 56], [30, 44, 56], [36, 46, 59], [37, 47, 58], [34, 50, 60]],
          [[34, 44, 54], [36, 48, 55], [38, 51, 59], [32, 47, 59], [38, 44, 54], [31, 44, 57], [37, 47, 55], [31, 50, 59]],
          [[36, 48, 58], [41, 50, 56], [42, 50, 61], [41, 54, 59], [40, 47, 61], [42, 53, 56], [37, 51, 58], [33, 53, 61]],
          [[39, 47, 55], [39, 47, 59], [36, 47, 57], [36, 50, 53], [33, 45, 55], [31, 46, 57], [32, 46, 53], [39, 49, 56]],
          [[35, 45, 55], [33, 45, 59], [29, 45, 55], [37, 45, 60], [34, 47, 58], [35, 48, 58], [33, 46, 55], [34, 44, 59]],
          [[41, 45, 55], [39, 51, 61], [38, 52, 56], [38, 47, 56], [47, 51, 54], [37, 48, 56], [40, 53, 58], [40, 50, 60]],
          [[37, 48, 56], [40, 48, 60], [36, 50, 58], [33, 45, 54], [33, 45, 60], [37, 47, 55], [37, 50, 55], [36, 48, 54]],
          [[35, 51, 58], [40, 49, 60], [38, 51, 58], [35, 48, 57], [42, 49, 61], [33, 49, 58], [37, 51, 57], [37, 50, 62]]]
TRIES = 40


def bits(engines):
    m = 0
    for e in engines:
        m |= 1 << e
    return m


def pack_once(items, load, rnd):
    groups = {}
    for it in items:
        groups.setdefault(it[0], []).append(it)
    chunks = []
    for w in sorted(groups):
        off = [it for it in groups[w] if it[5]]
        on = [it for it in groups[w] if not it[5]]
        cap = (16, 16, 12, 8)[rnd(4)]
        while off or on:
            a = off[:min(8, cap)]
            off = off[len(a):]
            b = on[:cap - len(a)]
            on = on[len(b):]
            chunks.append(a + b)
    chunks.sort(key=lambda c: -len(c) + rnd(5))
    calls = []
    for ch in chunks:
        free = set(range(16))
        got = []
        for it in ch:
            allowed = [e for e in free if (e < 8 or not it[5])]
            e = min(allowed, key=lambda e: (load[e], -e))
            free.discard(e)
            got.append([e])
        while free:
            best = None
            for i, it in enumerate(ch):
                m = len(got[i])
                allowed = sorted([e for e in free if (e < 8 or not it[5])], key=lambda e: (load[e], -e))
                if len(allowed) < m or m >= 16:
                    continue
                end = max(load[e] for e in got[i]) + 128 // m
                new = max(load[e] for e in got[i] + allowed[:m]) + 64 // m
                if new < end and (best is None or end > best[0]):
                    best = (end, i, allowed[:m])
            if best is None:
                break
            got[best[1]] += best[2]
            for e in best[2]:
                free.discard(e)
        for i, it in enumerate(ch):
            for e in got[i]:
                load[e] += 128 // len(got[i])
        calls.append([(got[i], ch[i]) for i in range(len(ch))])
    return calls


def dice(seed):
    state = [seed * 7919 + 1]

    def rnd(n):
        state[0] = (state[0] * 1103515245 + 12345) % 2147483648
        return (state[0] >> 8) % n

    return rnd


def pack(items, load0, tries):
    best = None
    for k in range(tries):
        load = list(load0)
        calls = pack_once(items, load, dice(k) if k else (lambda n: 0))
        score = max(load) + 4 * len(calls)
        if best is None or score < best[0]:
            best = (score, calls, load)
    return best[1], best[2]


def build(route, cores, splits, tries):
    n = len(cores)
    col = {}
    cnt = [0] * n
    for e in range(n):
        for r in range(n):
            for t in range(NT):
                if e in route[r][t]:
                    col[(r, t, e)] = cnt[e]
                    cnt[e] += 1

    def runs(r, e, lo, hi, buf, off):
        out = []
        t = lo
        while t < hi:
            if (r, t, e) in col:
                t0 = t
                while t < hi and (r, t, e) in col:
                    t += 1
                out.append((t - t0, buf, t0, cores[e], col[(r, t0, e)], off))
            else:
                t += 1
        return out

    prog = {}

    def core_of(h, k, chip=6):
        return cores[2 * h] - cores[2 * h] % 8 + (chip - 6) * 8 + k

    for h in range(4):
        for k in range(8):
            prog[core_of(h, k)] = {"items": [], "xin": 0, "sends": [], "load": [0] * 16, "A": 0}
            prog[core_of(h, k, 4)] = {"items": [], "xin": 0, "sends": [], "load": [0] * 16, "A": 0}
    HEAD = {(-1, 0): 0, (-1, 1): 4, (1, 0): 1, (1, 1): 6}
    TAIL = {0: 5, 1: 7}
    LO, HI, UP = (0, 1, 2, 3), (4, 5, 6, 7), tuple(range(8, 16))
    for r in range(n):
        hr, par = r // 2, r % 2
        me, partner = cores[r], cores[r ^ 1]
        hd, hc = (hr + 2) % 4, hr ^ 3
        need = {}

        def give(i, c, buf, e, lo, hi, off):
            prog[c]["items"] += runs(r, e, lo, hi, buf, off)
            a, b = need.get((i, c), (NT, 0))
            need[(i, c)] = (min(a, lo), max(b, hi))

        for e in range(n):
            he = e // 2
            s1, s2, s3 = splits[r][e]
            if he == hr:
                hold = [(partner, "xa") if e == r else (me, "xs"), (core_of(hr, TAIL[par]), "xb")]
                off = False
            else:
                h = he if he != hd else (hr + (1 if e % 2 == 0 else 3)) % 4
                d = 1 if h == (hr + 1) % 4 else -1
                hold = [(core_of(h, HEAD[(-d, par)]), "xa"), (core_of(h, TAIL[par]), "xa" if d == 1 else "xs")]
                off = he == hd
            hx, k0 = (hr, 0) if he // 2 == hr // 2 else (hc, 4)
            give(0, hold[0][0], hold[0][1], e, 0, s1, off)
            give(1, hold[1][0], hold[1][1], e, s1, s2, off)
            give(2, core_of(hx, k0 + 2 * par, 4), "xa", e, s2, s3, True)
            give(3, core_of(hx, k0 + 2 * par + 1, 4), "xa", e, s3, NT, True)
        hp, hm = (hr + 1) % 4, (hr + 3) % 4
        trs = [[(LO, "xa", core_of(hp, HEAD[(-1, par)])), (HI, "xa", core_of(hm, HEAD[(1, par)])), (UP, "xa", partner)],
               [(LO, "xa", core_of(hp, TAIL[par])), (HI, "xs", core_of(hm, TAIL[par])), (UP, "xb", core_of(hr, TAIL[par]))],
               [(LO, "xa", core_of(hr, 2 * par, 4)), (HI, "xa", core_of(hc, 4 + 2 * par, 4))],
               [(LO, "xa", core_of(hr, 2 * par + 1, 4)), (HI, "xa", core_of(hc, 5 + 2 * par, 4))]]
        sends = []
        for i in range(4):
            wid = max(need[(i, d)][1] - need[(i, d)][0] for eng, b, d in trs[i])
            sends.append([(eng, b, d, min(need[(i, d)][0], NT - wid), wid) for eng, b, d in trs[i]])
        prog[me]["sends"] = sends
        prog[me]["load"] = [128] * 8 + [32] * 8
        for i in range(4):
            for eng, b, d in trs[i]:
                prog[d]["xin"] += len(eng)
                if d != partner:
                    prog[d]["A"] = 32 * (i + 1)
    if not tries:
        return prog
    arr = {c: 0 for c in cores}
    for c in prog:
        p = prog[c]
        p["calls"], p["load"] = pack(p["items"], p["load"], tries)
        p["sent"] = sum(len(eng) for call in p["calls"] for eng, it in call)
        p["sent"] += sum(len(tr[0]) for trs in p["sends"] for tr in trs)
        for call in p["calls"]:
            for eng, it in call:
                arr[it[3]] += len(eng)
    for e in range(n):
        prog[cores[e]]["arr"] = arr[cores[e]]
        prog[cores[e]]["cnt"] = cnt[e]
    return prog


def rank_program(g, core, T, topo):
    if "p" not in PLAN:
        PLAN["p"] = build(T.tables["ROUTE"], list(T.cores), SPLITS, TRIES)
    p = PLAN["p"].get(core)
    if p is None:
        return
    sem = T.sem

    def dst(d):
        rid, pid = topo.addr(d, core)
        return DstId(rid=rid, pnc=pid)

    rank = T.rank_of(core)
    if rank is not None:
        g.sync.dma_start(T.xs[:], T.x[:]).then_inc(sem.ld, 16)
        g.wait_ge(sem.ld, 16)
        for trs in p["sends"]:
            g.remote_dma_fused(
                [RemoteDMATransfer(dst_ids=[dst(d)], dma_engine_mask=bits(eng), remote_sem=sem.xin,
                                   src=T.xs[:, lo:lo + w], dst=T[b][:, lo:lo + w]) for eng, b, d, lo, w in trs],
                local_sem=sem.sent)
    g.wait_ge(sem.xin, p["xin"])
    for call in p["calls"]:
        g.remote_dma_fused(
            [RemoteDMATransfer(dst_ids=[dst(it[3])], dma_engine_mask=bits(eng), remote_sem=sem.arr,
                               src=T[it[1]][:, it[2]:it[2] + it[0]], dst=T.land[:, it[4]:it[4] + it[0]])
             for eng, it in call],
            local_sem=sem.sent)
    if rank is not None:
        n = p["cnt"]
        g.sync.wait_ge(sem.arr, p["arr"])
        g.sync.dma_start(T.y[:, 0:n], T.land[:, 0:n]).then_inc(sem.st, 16)
        g.wait_ge(sem.arr, p["arr"])
        g.wait_ge(sem.st, 16)
    g.wait_ge(sem.sent, p["sent"])
